import numpy as np
import ml_dtypes


def mxq(x, axis, fmt="e4m3"):
    dtype, down = {"e4m3": (ml_dtypes.float8_e4m3fn, 7), "e5m2": (ml_dtypes.float8_e5m2, 14)}[fmt]
    v = np.moveaxis(np.asarray(x, np.float32).astype(ml_dtypes.bfloat16).astype(np.float64), axis, -1)
    blocks = v.reshape(v.shape[:-1] + (-1, 32))
    amax = np.abs(blocks).max(-1, keepdims=True)
    byte = np.maximum(np.where(amax > 0, np.frexp(amax)[1] - 1 + 127, 0) - down, 1)
    scale = np.exp2(byte - 127.0)
    codes = (blocks / scale).astype(np.float32).astype(dtype).astype(np.float64)
    return np.moveaxis((codes * scale).reshape(v.shape), -1, axis)


WIDE = False


def mx_kscale(k):
    if not WIDE:
        return np.ones(k)
    levels = np.array([30, -30])
    if k % 512:
        return np.exp2(np.random.permutation(np.resize(levels, k // 32))).repeat(32)
    a = np.empty((k // 512, 16))
    for p in range(k // 512):
        a[p, :8] = np.random.permutation(np.resize(levels, 8))
        for g in range(8):
            far = levels[np.abs(levels - a[p, g]) >= 10]
            a[p, g + 8] = far[np.random.randint(len(far))]
    return np.exp2(a.ravel()).repeat(32)


def f64(x):
    return np.asarray(x).astype(np.float64)


def striped(idx):
    return np.tile(np.asarray(idx).reshape(-1, 16).T, (8, 1)).astype(np.uint16)


def unstriped(offs):
    return offs[:16].T.reshape(-1).astype(np.int64)


E2M1 = np.array([0.0, 0.5, 1.0, 1.5, 2.0, 3.0, 4.0, 6.0, -0.0, -0.5, -1.0, -1.5, -2.0, -3.0, -4.0, -6.0])


def pack_weight(w, fmt):
    k, n = w.shape
    w = f64(np.asarray(w, np.float32).astype(ml_dtypes.bfloat16)).reshape(k // 32, 32, n)
    amax = np.abs(w).max(1)
    if fmt == "e4m3":
        byte = np.frexp(amax)[1] - 1 + 127 - 7
    else:
        mant, ex = np.frexp(amax / 6.0)
        byte = np.where(mant > 0.5, ex, ex - 1) + 127
    byte = np.clip(np.where(amax > 0, byte, 1), 1, 254)
    scaled = (w * np.exp2(127.0 - byte)[:, None, :]).reshape(k, n).astype(np.float32)
    by_word = np.ascontiguousarray(scaled.reshape(k // 512, 128, 4, n).transpose(0, 1, 3, 2))
    if fmt == "e4m3":
        words = by_word.astype(ml_dtypes.float8_e4m3fn).view(np.uint8)
    else:
        c = by_word.astype(ml_dtypes.float4_e2m1fn).view(np.uint8) & 0xF
        words = (c[..., 0::2] | (c[..., 1::2] << 4)).reshape(k // 512, 128, 2 * n)
    return np.ascontiguousarray(words), np.ascontiguousarray(byte.astype(np.uint8).reshape(k // 512, 16, n))


def unpack_weight(words, scales, fmt):
    g, _, n = scales.shape
    words = np.ascontiguousarray(words).reshape(g, 128, n, -1)
    if fmt == "e4m3":
        vals = words.view(ml_dtypes.float8_e4m3fn).astype(np.float64)
    else:
        nib = np.empty((g, 128, n, 4), np.uint8)
        nib[..., 0::2] = words & 0xF
        nib[..., 1::2] = words >> 4
        vals = E2M1[nib]
    vals = vals * np.repeat(np.exp2(scales.astype(np.float64) - 127.0), 8, axis=1)[..., None]
    return vals.transpose(0, 1, 3, 2).reshape(g * 512, n)


def sigmoid(v):
    return 1.0 / (1.0 + np.exp(-v))


K, T, Z, J, R, Q, N, S, E = 512, 1024, 1024, 256, 512, 1024, 256, 1024, 1024


def setup_inputs():
    n = np.random.standard_normal
    idx = np.random.permutation(T)[:J]
    idx2 = np.random.permutation(Z)[:J]
    idx3 = np.random.permutation(J)[:J]
    idx4 = np.random.permutation(Q)[:J]
    idx5 = np.random.permutation(S)[:N]
    idx6 = np.random.permutation(E)[:J]
    fk = mx_kscale(K)
    fr = mx_kscale(R)
    xtp = pack_weight(n((K, T)) / fk[:, None], "e2m1")
    xop = pack_weight(n((K, Z)) / fk[:, None], "e4m3")
    wp = pack_weight(n((K, R)) * 1 / np.sqrt(K) * fk[:, None] * fr, "e4m3")
    vsp = pack_weight(n((R, S)) * 1 / np.sqrt(R) / fr[:, None], "e2m1")
    return {
        "xt_words": xtp[0],
        "xt_scales": xtp[1],
        "xo_words": xop[0],
        "xo_scales": xop[1],
        "w_words": wp[0],
        "w_scales": wp[1],
        "tg": (1.0 * n((R, Q))).astype(np.float32),
        "sg": (np.random.uniform(0.6, 1.6, (R, 1))).astype(np.float32),
        "bg": (np.random.uniform(-1.0, 1.0, (R, 1))).astype(np.float32),
        "vs_words": vsp[0],
        "vs_scales": vsp[1],
        "offs": striped(idx),
        "offs2": striped(idx2),
        "offs3": striped(idx3),
        "offs4": striped(idx4),
        "offs5": striped(idx5),
        "offs6": striped(idx6),
    }


def reference(xt_words, xt_scales, xo_words, xo_scales, w_words, w_scales, tg, sg, bg, vs_words, vs_scales, offs, offs2, offs3, offs4, offs5, offs6):
    idx = unstriped(offs)
    idx2 = unstriped(offs2)
    idx3 = unstriped(offs3)
    idx4 = unstriped(offs4)
    idx5 = unstriped(offs5)
    idx6 = unstriped(offs6)
    xtu = unpack_weight(xt_words, xt_scales, "e2m1")
    xou = unpack_weight(xo_words, xo_scales, "e4m3")
    wu = unpack_weight(w_words, w_scales, "e4m3")
    vsu = unpack_weight(vs_words, vs_scales, "e2m1")
    xtidxg = xtu[:, idx]
    a = wu.T @ xtidxg
    xoidx2g = xou[:, idx2]
    b = wu.T @ xoidx2g
    hid = np.abs(a - b[:, idx3]) * sigmoid(f64(tg)[:, idx4] * f64(sg) + f64(bg))
    vsidx5g = vsu[:, idx5]
    hidq = mxq(hid, 0, "e5m2")
    p = vsidx5g.T @ hidq
    y = np.zeros((N, E))
    y[:, idx6] = p
    return y

@@ -1,0 +1,199 @@
+from contextlib import ExitStack
+
+import concourse.mybir as mybir
+
+F32 = mybir.dt.float32
+BF16 = mybir.dt.bfloat16
+I32 = mybir.dt.int32
+U32 = mybir.dt.uint32
+U16 = mybir.dt.uint16
+U8 = mybir.dt.uint8
+E4M3 = mybir.dt.float8_e4m3fn_x4
+E5M2 = mybir.dt.float8_e5m2_x4
+E2M1 = mybir.dt.float4_e2m1fn_x4
+ACT = mybir.ActivationFunctionType
+ALU = mybir.AluOpType
+
+P = 128
+PACK = 4
+TABLE = 1024
+SLOTS = 256
+HIDDEN = 512
+OUT_ROWS = 256
+SPARE = 96
+FLOPS = 2 * 2 * 512 * HIDDEN * SLOTS + 2 * HIDDEN * OUT_ROWS * SLOTS
+
+
+def tile_list_tablepartner_oneforboth_store_scattered_kernel(
+    tc, xt_words, xt_scales, xo_words, xo_scales, w_words, w_scales, tg, sg, bg,
+    vs_words, vs_scales, offs, offs2, offs3, offs4, offs5, offs6, out,
+):
+    nc = tc.nc
+    with ExitStack() as ctx:
+        lists = ctx.enter_context(tc.tile_pool(name="lists", bufs=1))
+        keep = ctx.enter_context(tc.tile_pool(name="keep", bufs=1))
+        psum = ctx.enter_context(tc.psum_pool(name="psum", bufs=1))
+
+        def load_list(source, name):
+            tile = lists.tile([P, SLOTS // 16], U16, name=name)
+            nc.sync.dma_start(tile[:], source)
+            return tile
+
+        def zeroed_plane(width, name):
+            plane = keep.tile([P, width], U8, name=name, align_bytes=64)
+            nc.vector.memset(plane[:].bitcast(I32), 0)
+            return plane
+
+        def load_scale_rows(plane, source, queue):
+            for quad in range(4):
+                queue.dma_start(
+                    plane[32 * quad : 32 * quad + 4, :].bitcast(I32),
+                    source[0, 4 * quad : 4 * quad + 4, :].bitcast(I32),
+                )
+
+        xo_plane = zeroed_plane(TABLE, "xo_plane")
+        w_plane = zeroed_plane(HIDDEN, "w_plane")
+        xt_plane = zeroed_plane(TABLE, "xt_plane")
+        vs_plane = zeroed_plane(TABLE, "vs_plane")
+
+        tg_rows = tg.rearrange("(p t) q -> t p q", t=PACK)
+        tg_tiles = [keep.tile([P, TABLE], F32, name="tg%d" % t) for t in range(PACK)]
+        slope = keep.tile([P, PACK], F32, name="slope")
+        offset = keep.tile([P, PACK], F32, name="offset")
+        nc.gpsimd.dma_start(slope[:], sg.rearrange("(p t) o -> p (t o)", t=PACK))
+        nc.gpsimd.dma_start(offset[:], bg.rearrange("(p t) o -> p (t o)", t=PACK))
+        load_scale_rows(vs_plane, vs_scales, nc.gpsimd)
+
+        xo_tab = keep.tile([P, TABLE], U32, name="xo_tab", align_bytes=64)
+        w_tab = keep.tile([P, HIDDEN], U32, name="w_tab", align_bytes=64)
+        xt_tab = keep.tile([P, TABLE], U16, name="xt_tab", align_bytes=64)
+        vs_tab = keep.tile([P, TABLE], U16, name="vs_tab", align_bytes=64)
+
+        xo_list = load_list(offs2, "xo_list")
+        nc.sync.dma_start(xo_tab[:].bitcast(I32), xo_words[0].rearrange("p n t -> p (n t)").bitcast(I32))
+        load_scale_rows(xo_plane, xo_scales, nc.scalar)
+        nc.sync.dma_start(w_tab[:].bitcast(I32), w_words[0].rearrange("p n t -> p (n t)").bitcast(I32))
+        nc.sync.dma_start(tg_tiles[0][:], tg_rows[0])
+        load_scale_rows(w_plane, w_scales, nc.sync)
+        tg_list = load_list(offs4, "tg_list")
+        nc.sync.dma_start(xt_tab[:].bitcast(I32), xt_words[0].bitcast(I32))
+        xt_list = load_list(offs, "xt_list")
+        nc.sync.dma_start(tg_tiles[1][:], tg_rows[1])
+        load_scale_rows(xt_plane, xt_scales, nc.sync)
+        partner_list = load_list(offs3, "partner_list")
+        nc.sync.dma_start(tg_tiles[2][:], tg_rows[2])
+        nc.sync.dma_start(tg_tiles[3][:], tg_rows[3])
+        nc.sync.dma_start(vs_tab[:].bitcast(I32), vs_words[0].bitcast(I32))
+        vs_list = load_list(offs5, "vs_list")
+        page_list = load_list(offs6, "page_list")
+
+        b_pairs = [keep.tile([P, 2 * SLOTS + SPARE], F32, name="b_pair%d" % u) for u in range(2)]
+        pages = [keep.tile([P, TABLE], F32, name="page%d" % h) for h in range(2)]
+        for u in range(2):
+            nc.vector.memset(b_pairs[u][:, 2 * SLOTS :], 0.0)
+        for h in range(2):
+            nc.vector.memset(pages[h][:], 0.0)
+
+        def pick(table, offsets, dtype, name):
+            picked = keep.tile([P, SLOTS], dtype, name=name, align_bytes=64)
+            nc.vector.tensor_copy(picked[:], table[:].indirect(offsets[:]))
+            return picked
+
+        gate = keep.tile([P, PACK, SLOTS], F32, name="gate")
+
+        def look_gate(t):
+            nc.scalar.activation(
+                out=gate[:, t, :], in_=tg_tiles[t][:].indirect(tg_list[:]), func=ACT.Sigmoid,
+                bias=offset[:, t : t + 1], scale=slope[:, t : t + 1],
+            )
+
+        look_gate(0)
+
+        xo_codes = pick(xo_tab, xo_list, U32, "xo_codes")
+        xo_bytes = pick(xo_plane, xo_list, U8, "xo_bytes")
+
+        w_codes = keep.tile([P, HIDDEN], U32, name="w_codes", align_bytes=64)
+        w_bytes = keep.tile([P, HIDDEN], U8, name="w_bytes", align_bytes=64)
+        nc.vector.tensor_copy(
+            w_codes[:].rearrange("p (t c i) -> p c t i", t=PACK, i=4),
+            w_tab[:].rearrange("p (c i t) -> p c t i", t=PACK, i=4),
+        )
+        nc.vector.tensor_copy(
+            w_bytes[:].rearrange("p (t c i) -> p c t i", t=PACK, i=16),
+            w_plane[:].rearrange("p (c i t) -> p c t i", t=PACK, i=16),
+        )
+
+        def first_product(codes, scale_bytes, name):
+            banks = [psum.tile([P, 2, SLOTS], F32, name="%s%d" % (name, u)) for u in range(2)]
+            for t in range(PACK):
+                nc.tensor.matmul_mx(
+                    out=banks[t // 2][:, t % 2, :],
+                    lhsT=w_codes[:, t * P : (t + 1) * P].bitcast(E4M3),
+                    lhsT_scale=w_bytes[:, t * P : (t + 1) * P],
+                    rhs=codes, rhs_scale=scale_bytes[:], start=True, stop=True,
+                )
+            return banks
+
+        b_banks = first_product(xo_codes[:].bitcast(E4M3), xo_bytes, "b_bank")
+        for u in range(2):
+            nc.scalar.copy(b_pairs[u][:, : 2 * SLOTS], b_banks[u][:].rearrange("p t j -> p (t j)"))
+
+        xt_codes = pick(xt_tab, xt_list, U16, "xt_codes")
+        xt_bytes = pick(xt_plane, xt_list, U8, "xt_bytes")
+        a_banks = first_product(xt_codes[:].bitcast(E2M1), xt_bytes, "a_bank")
+
+        look_gate(1)
+
+        partner = keep.tile([P, PACK, SLOTS], F32, name="partner")
+        diff = keep.tile([P, PACK, SLOTS], F32, name="diff")
+        size = keep.tile([P, PACK, SLOTS], F32, name="size")
+        hid = keep.tile([P, SLOTS, PACK], BF16, name="hid", align_bytes=64)
+        for t in range(PACK):
+            start = (t % 2) * SLOTS
+            width = SLOTS + SPARE if t % 2 else 2 * SLOTS
+            window = b_pairs[t // 2][:, start : start + width].indirect(partner_list[:])
+            if t == 2:
+                nc.scalar.activation(out=partner[:, t, :], in_=window, func=ACT.Copy)
+            else:
+                nc.vector.tensor_copy(partner[:, t, :], window)
+        for u in range(2):
+            pair = slice(2 * u, 2 * u + 2)
+            nc.vector.tensor_tensor(diff[:, pair, :], a_banks[u][:], partner[:, pair, :], ALU.subtract)
+            look_gate(2 + u)
+            nc.scalar.activation(out=size[:, pair, :], in_=diff[:, pair, :], func=ACT.Abs)
+
+        vs_codes = pick(vs_tab, vs_list, U16, "vs_codes")
+        vs_bytes = pick(vs_plane, vs_list, U8, "vs_bytes")
+
+        for u in range(2):
+            pair = slice(2 * u, 2 * u + 2)
+            nc.vector.tensor_tensor(
+                hid[:, :, pair],
+                size[:, pair, :].rearrange("p t j -> p j t"),
+                gate[:, pair, :].rearrange("p t j -> p j t"),
+                ALU.mult,
+            )
+
+        hid_codes = keep.tile([P, SLOTS], U32, name="hid_codes", align_bytes=64)
+        hid_bytes = keep.tile([P, SLOTS], U8, name="hid_bytes", align_bytes=64)
+        nc.vector.quantize_mx(
+            out=hid_codes[:].bitcast(E5M2), scales=hid_bytes[:], in_=hid[:].rearrange("p j t -> p (j t)")
+        )
+
+        for h in range(2):
+            rows = slice(h * P, (h + 1) * P)
+            p_bank = psum.tile([P, SLOTS], F32, name="p_bank%d" % h)
+            nc.tensor.matmul_mx(
+                out=p_bank[:], lhsT=vs_codes[:, rows].bitcast(E2M1), lhsT_scale=vs_bytes[:, rows],
+                rhs=hid_codes[:].bitcast(E5M2), rhs_scale=hid_bytes[:], start=True, stop=True,
+            )
+            result = keep.tile([P, SLOTS], F32, name="result%d" % h)
+            placed = pages[h][:].indirect(page_list[:])
+            if h == 0:
+                nc.vector.tensor_copy(result[:], p_bank[:])
+                nc.vector.tensor_copy(placed, result[:])
+                nc.sync.dma_start(out[rows, :], pages[h][:])
+            else:
+                nc.scalar.copy(result[:], p_bank[:])
+                nc.scalar.activation(out=placed, in_=result[:], func=ACT.Copy)
+                nc.scalar.dma_start(out[rows, :], pages[h][:])

@@ -20,7 +20,8 @@ TABLE = 1024
 SLOTS = 256
 HIDDEN = 512
 OUT_ROWS = 256
-SPARE = 96
+SPARE = (96, 256)
+GATE_TAG = ("xo_codes", "b_pair0")
 FLOPS = 2 * 2 * 512 * HIDDEN * SLOTS + 2 * HIDDEN * OUT_ROWS * SLOTS
 
 
@@ -44,15 +45,15 @@ def tile_list_tablepartner_oneforboth_store_scattered_kernel(
             nc.vector.memset(plane[:].bitcast(I32), 0)
             return plane
 
-        def load_scale_rows(plane, source, queue):
-            for quad in range(4):
-                queue.dma_start(
+        def load_scale_rows(plane, source, quads):
+            for quad in quads:
+                nc.sync.dma_start(
                     plane[32 * quad : 32 * quad + 4, :].bitcast(I32),
                     source[0, 4 * quad : 4 * quad + 4, :].bitcast(I32),
                 )
 
-        xo_plane = zeroed_plane(TABLE, "xo_plane")
         w_plane = zeroed_plane(HIDDEN, "w_plane")
+        xo_plane = zeroed_plane(TABLE, "xo_plane")
         xt_plane = zeroed_plane(TABLE, "xt_plane")
         vs_plane = zeroed_plane(TABLE, "vs_plane")
 
@@ -62,52 +63,51 @@ def tile_list_tablepartner_oneforboth_store_scattered_kernel(
         offset = keep.tile([P, PACK], F32, name="offset")
         nc.gpsimd.dma_start(slope[:], sg.rearrange("(p t) o -> p (t o)", t=PACK))
         nc.gpsimd.dma_start(offset[:], bg.rearrange("(p t) o -> p (t o)", t=PACK))
-        load_scale_rows(vs_plane, vs_scales, nc.gpsimd)
+        for t in range(PACK):
+            nc.gpsimd.dma_start(tg_tiles[t][:], tg_rows[t])
 
         xo_tab = keep.tile([P, TABLE], U32, name="xo_tab", align_bytes=64)
         w_tab = keep.tile([P, HIDDEN], U32, name="w_tab", align_bytes=64)
         xt_tab = keep.tile([P, TABLE], U16, name="xt_tab", align_bytes=64)
         vs_tab = keep.tile([P, TABLE], U16, name="vs_tab", align_bytes=64)
 
-        xo_list = load_list(offs2, "xo_list")
-        nc.sync.dma_start(xo_tab[:].bitcast(I32), xo_words[0].rearrange("p n t -> p (n t)").bitcast(I32))
-        load_scale_rows(xo_plane, xo_scales, nc.scalar)
         nc.sync.dma_start(w_tab[:].bitcast(I32), w_words[0].rearrange("p n t -> p (n t)").bitcast(I32))
-        nc.sync.dma_start(tg_tiles[0][:], tg_rows[0])
-        load_scale_rows(w_plane, w_scales, nc.sync)
+        xo_list = load_list(offs2, "xo_list")
         tg_list = load_list(offs4, "tg_list")
-        nc.sync.dma_start(xt_tab[:].bitcast(I32), xt_words[0].bitcast(I32))
         xt_list = load_list(offs, "xt_list")
-        nc.sync.dma_start(tg_tiles[1][:], tg_rows[1])
-        load_scale_rows(xt_plane, xt_scales, nc.sync)
+        load_scale_rows(w_plane, w_scales, range(2))
+        nc.sync.dma_start(xo_tab[:].bitcast(I32), xo_words[0].rearrange("p n t -> p (n t)").bitcast(I32))
+        nc.sync.dma_start(xt_tab[:].bitcast(I32), xt_words[0].bitcast(I32))
+        load_scale_rows(w_plane, w_scales, range(2, 4))
+        load_scale_rows(xo_plane, xo_scales, range(4))
         partner_list = load_list(offs3, "partner_list")
-        nc.sync.dma_start(tg_tiles[2][:], tg_rows[2])
-        nc.sync.dma_start(tg_tiles[3][:], tg_rows[3])
-        nc.sync.dma_start(vs_tab[:].bitcast(I32), vs_words[0].bitcast(I32))
         vs_list = load_list(offs5, "vs_list")
+        load_scale_rows(xt_plane, xt_scales, range(4))
+        nc.sync.dma_start(vs_tab[:].bitcast(I32), vs_words[0].bitcast(I32))
         page_list = load_list(offs6, "page_list")
+        load_scale_rows(vs_plane, vs_scales, range(4))
 
-        b_pairs = [keep.tile([P, 2 * SLOTS + SPARE], F32, name="b_pair%d" % u) for u in range(2)]
+        b_pairs = [
+            keep.tile([P, 2 * SLOTS + SPARE[u]], F32, name="b_pair%d" % u, tag="b_pair%d" % u, align_bytes=64)
+            for u in range(2)
+        ]
         pages = [keep.tile([P, TABLE], F32, name="page%d" % h) for h in range(2)]
-        for u in range(2):
-            nc.vector.memset(b_pairs[u][:, 2 * SLOTS :], 0.0)
         for h in range(2):
-            nc.vector.memset(pages[h][:], 0.0)
+            nc.vector.memset(pages[h][:, :511], 0.0)
+            nc.vector.memset(pages[h][:, 511:], 0.0)
+        for u in range(2):
+            nc.scalar.activation(out=b_pairs[u][:, 2 * SLOTS :], in_=pages[0][:, : SPARE[u]], func=ACT.Sigmoid)
 
-        def pick(table, offsets, dtype, name):
-            picked = keep.tile([P, SLOTS], dtype, name=name, align_bytes=64)
+        def pick(table, offsets, dtype, name, tag=None):
+            picked = keep.tile([P, SLOTS], dtype, name=name, tag=tag or name, align_bytes=64)
             nc.vector.tensor_copy(picked[:], table[:].indirect(offsets[:]))
             return picked
 
-        gate = keep.tile([P, PACK, SLOTS], F32, name="gate")
-
-        def look_gate(t):
+        def look_gate(t, gate):
             nc.scalar.activation(
-                out=gate[:, t, :], in_=tg_tiles[t][:].indirect(tg_list[:]), func=ACT.Sigmoid,
+                out=gate, in_=tg_tiles[t][:].indirect(tg_list[:]), func=ACT.Sigmoid,
                 bias=offset[:, t : t + 1], scale=slope[:, t : t + 1],
             )
-
-        look_gate(0)
 
         xo_codes = pick(xo_tab, xo_list, U32, "xo_codes")
         xo_bytes = pick(xo_plane, xo_list, U8, "xo_bytes")
@@ -136,41 +136,47 @@ def tile_list_tablepartner_oneforboth_store_scattered_kernel(
 
         b_banks = first_product(xo_codes[:].bitcast(E4M3), xo_bytes, "b_bank")
         for u in range(2):
-            nc.scalar.copy(b_pairs[u][:, : 2 * SLOTS], b_banks[u][:].rearrange("p t j -> p (t j)"))
+            nc.scalar.activation(
+                out=b_pairs[u][:, : 2 * SLOTS], in_=b_banks[u][:].rearrange("p t j -> p (t j)"), func=ACT.Copy
+            )
 
         xt_codes = pick(xt_tab, xt_list, U16, "xt_codes")
         xt_bytes = pick(xt_plane, xt_list, U8, "xt_bytes")
         a_banks = first_product(xt_codes[:].bitcast(E2M1), xt_bytes, "a_bank")
 
-        look_gate(1)
-
-        partner = keep.tile([P, PACK, SLOTS], F32, name="partner")
-        diff = keep.tile([P, PACK, SLOTS], F32, name="diff")
-        size = keep.tile([P, PACK, SLOTS], F32, name="size")
         hid = keep.tile([P, SLOTS, PACK], BF16, name="hid", align_bytes=64)
-        for t in range(PACK):
-            start = (t % 2) * SLOTS
-            width = SLOTS + SPARE if t % 2 else 2 * SLOTS
-            window = b_pairs[t // 2][:, start : start + width].indirect(partner_list[:])
-            if t == 2:
-                nc.scalar.activation(out=partner[:, t, :], in_=window, func=ACT.Copy)
-            else:
-                nc.vector.tensor_copy(partner[:, t, :], window)
+        partners, diffs, sizes, gates = [], [], [], []
         for u in range(2):
-            pair = slice(2 * u, 2 * u + 2)
-            nc.vector.tensor_tensor(diff[:, pair, :], a_banks[u][:], partner[:, pair, :], ALU.subtract)
-            look_gate(2 + u)
-            nc.scalar.activation(out=size[:, pair, :], in_=diff[:, pair, :], func=ACT.Abs)
+            partner = keep.tile([P, 2, SLOTS], F32, name="partner%d" % u, tag="partner%d" % u, align_bytes=64)
+            for e in range(2):
+                width = SLOTS + SPARE[u] if e else 2 * SLOTS
+                window = b_pairs[u][:, e * SLOTS : e * SLOTS + width].indirect(partner_list[:])
+                if u:
+                    nc.scalar.activation(out=partner[:, e, :], in_=window, func=ACT.Copy)
+                else:
+                    nc.vector.tensor_copy(partner[:, e, :], window)
+            partners.append(partner)
+        for u in range(2):
+            diff = keep.tile([P, 2, SLOTS], F32, name="diff%d" % u)
+            nc.vector.tensor_tensor(diff[:], a_banks[u][:], partners[u][:], ALU.subtract)
+            diffs.append(diff)
+        for u in range(2):
+            gate = keep.tile([P, 2, SLOTS], F32, name="gate%d" % u, tag=GATE_TAG[u], align_bytes=64)
+            for e in range(2):
+                look_gate(2 * u + e, gate[:, e, :])
+            gates.append(gate)
+            size = keep.tile([P, 2, SLOTS], F32, name="size%d" % u)
+            nc.scalar.activation(out=size[:], in_=diffs[u][:], func=ACT.Abs)
+            sizes.append(size)
 
-        vs_codes = pick(vs_tab, vs_list, U16, "vs_codes")
-        vs_bytes = pick(vs_plane, vs_list, U8, "vs_bytes")
+        vs_codes = pick(vs_tab, vs_list, U16, "vs_codes", "partner0")
+        vs_bytes = pick(vs_plane, vs_list, U8, "vs_bytes", "xt_bytes")
 
         for u in range(2):
-            pair = slice(2 * u, 2 * u + 2)
             nc.vector.tensor_tensor(
-                hid[:, :, pair],
-                size[:, pair, :].rearrange("p t j -> p j t"),
-                gate[:, pair, :].rearrange("p t j -> p j t"),
+                hid[:, :, 2 * u : 2 * u + 2],
+                sizes[u][:].rearrange("p t j -> p j t"),
+                gates[u][:].rearrange("p t j -> p j t"),
                 ALU.mult,
             )
 

@@ -16,13 +16,16 @@ ALU = mybir.AluOpType
 
 P = 128
 PACK = 4
+FEATURES = 512
 TABLE = 1024
 SLOTS = 256
 HIDDEN = 512
 OUT_ROWS = 256
-SPARE = (96, 256)
-GATE_TAG = ("xo_codes", "b_pair0")
-FLOPS = 2 * 2 * 512 * HIDDEN * SLOTS + 2 * HIDDEN * OUT_ROWS * SLOTS
+HALF = SLOTS // 2
+LINE = 16
+SPARE = (SLOTS, 96)
+PAGE_CUT = TABLE // 2 - 1
+FLOPS = 2 * 2 * FEATURES * HIDDEN * SLOTS + 2 * HIDDEN * OUT_ROWS * SLOTS
 
 
 def tile_list_tablepartner_oneforboth_store_scattered_kernel(
@@ -35,101 +38,102 @@ def tile_list_tablepartner_oneforboth_store_scattered_kernel(
         keep = ctx.enter_context(tc.tile_pool(name="keep", bufs=1))
         psum = ctx.enter_context(tc.psum_pool(name="psum", bufs=1))
 
-        def load_list(source, name):
-            tile = lists.tile([P, SLOTS // 16], U16, name=name)
-            nc.sync.dma_start(tile[:], source)
-            return tile
+        def tile(shape, dtype, name, tag=None):
+            return keep.tile(shape, dtype, name=name, tag=tag or name, align_bytes=64)
 
-        def zeroed_plane(width, name):
-            plane = keep.tile([P, width], U8, name=name, align_bytes=64)
-            nc.vector.memset(plane[:].bitcast(I32), 0)
+        def load_list(source, name):
+            entries = lists.tile([P, SLOTS // 16], U16, name=name)
+            nc.sync.dma_start(entries[:], source)
+            return entries
+
+        def zeroed_plane(width, name, engine, tag=None):
+            plane = tile([P, width], U8, name, tag)
+            engine.memset(plane[:].bitcast(I32), 0)
             return plane
 
-        def load_scale_rows(plane, source, quads):
-            for quad in quads:
+        def load_scale_rows(plane, source):
+            for quad in range(4):
                 nc.sync.dma_start(
                     plane[32 * quad : 32 * quad + 4, :].bitcast(I32),
                     source[0, 4 * quad : 4 * quad + 4, :].bitcast(I32),
                 )
 
-        w_plane = zeroed_plane(HIDDEN, "w_plane")
-        xo_plane = zeroed_plane(TABLE, "xo_plane")
-        xt_plane = zeroed_plane(TABLE, "xt_plane")
-        vs_plane = zeroed_plane(TABLE, "vs_plane")
+        def load_words(table, source):
+            nc.sync.dma_start(table[:].bitcast(I32), source.bitcast(I32))
+
+        xo_plane = zeroed_plane(TABLE, "xo_plane", nc.gpsimd)
+        w_plane = zeroed_plane(HIDDEN, "w_plane", nc.gpsimd)
+        xt_plane = zeroed_plane(TABLE, "xt_plane", nc.vector, "after_xt")
+        vs_plane = zeroed_plane(TABLE, "vs_plane", nc.vector)
 
         tg_rows = tg.rearrange("(p t) q -> t p q", t=PACK)
-        tg_tiles = [keep.tile([P, TABLE], F32, name="tg%d" % t) for t in range(PACK)]
-        slope = keep.tile([P, PACK], F32, name="slope")
-        offset = keep.tile([P, PACK], F32, name="offset")
+        tg_tiles = [tile([P, TABLE], F32, "tg%d" % t) for t in range(PACK)]
+        slope = tile([P, PACK], F32, "slope")
+        shift = tile([P, PACK], F32, "shift")
         nc.gpsimd.dma_start(slope[:], sg.rearrange("(p t) o -> p (t o)", t=PACK))
-        nc.gpsimd.dma_start(offset[:], bg.rearrange("(p t) o -> p (t o)", t=PACK))
-        for t in range(PACK):
-            nc.gpsimd.dma_start(tg_tiles[t][:], tg_rows[t])
+        nc.gpsimd.dma_start(shift[:], bg.rearrange("(p t) o -> p (t o)", t=PACK))
 
-        xo_tab = keep.tile([P, TABLE], U32, name="xo_tab", align_bytes=64)
-        w_tab = keep.tile([P, HIDDEN], U32, name="w_tab", align_bytes=64)
-        xt_tab = keep.tile([P, TABLE], U16, name="xt_tab", align_bytes=64)
-        vs_tab = keep.tile([P, TABLE], U16, name="vs_tab", align_bytes=64)
+        xo_tab = tile([P, TABLE], U32, "xo_tab")
+        w_tab = tile([P, HIDDEN], U32, "w_tab")
+        xt_tab = tile([P, TABLE], U16, "xt_tab")
+        vs_tab = tile([P, TABLE], U16, "vs_tab", "after_vs")
 
-        nc.sync.dma_start(w_tab[:].bitcast(I32), w_words[0].rearrange("p n t -> p (n t)").bitcast(I32))
         xo_list = load_list(offs2, "xo_list")
-        tg_list = load_list(offs4, "tg_list")
+        load_scale_rows(xo_plane, xo_scales)
+        load_words(xo_tab, xo_words[0].rearrange("p n t -> p (n t)"))
+        load_words(w_tab, w_words[0].rearrange("p n t -> p (n t)"))
         xt_list = load_list(offs, "xt_list")
-        load_scale_rows(w_plane, w_scales, range(2))
-        nc.sync.dma_start(xo_tab[:].bitcast(I32), xo_words[0].rearrange("p n t -> p (n t)").bitcast(I32))
-        nc.sync.dma_start(xt_tab[:].bitcast(I32), xt_words[0].bitcast(I32))
-        load_scale_rows(w_plane, w_scales, range(2, 4))
-        load_scale_rows(xo_plane, xo_scales, range(4))
+        load_scale_rows(w_plane, w_scales)
+        nc.sync.dma_start(tg_tiles[0][:], tg_rows[0])
+        load_words(xt_tab, xt_words[0])
         partner_list = load_list(offs3, "partner_list")
+        load_scale_rows(xt_plane, xt_scales)
+        nc.sync.dma_start(tg_tiles[1][:], tg_rows[1])
+        tg_list = load_list(offs4, "tg_list")
+        nc.sync.dma_start(tg_tiles[2][:], tg_rows[2])
+        load_words(vs_tab, vs_words[0])
         vs_list = load_list(offs5, "vs_list")
-        load_scale_rows(xt_plane, xt_scales, range(4))
-        nc.sync.dma_start(vs_tab[:].bitcast(I32), vs_words[0].bitcast(I32))
+        load_scale_rows(vs_plane, vs_scales)
+        nc.sync.dma_start(tg_tiles[3][:], tg_rows[3])
         page_list = load_list(offs6, "page_list")
-        load_scale_rows(vs_plane, vs_scales, range(4))
 
-        b_pairs = [
-            keep.tile([P, 2 * SLOTS + SPARE[u]], F32, name="b_pair%d" % u, tag="b_pair%d" % u, align_bytes=64)
-            for u in range(2)
-        ]
-        pages = [keep.tile([P, TABLE], F32, name="page%d" % h) for h in range(2)]
+        b_pairs = [tile([P, 2 * SLOTS + SPARE[u]], F32, "b_pair%d" % u) for u in range(2)]
+        pages = [tile([P, TABLE], F32, "page%d" % h) for h in range(2)]
         for h in range(2):
-            nc.vector.memset(pages[h][:, :511], 0.0)
-            nc.vector.memset(pages[h][:, 511:], 0.0)
+            nc.vector.memset(pages[h][:, :PAGE_CUT], 0.0)
+            nc.vector.memset(pages[h][:, PAGE_CUT:], 0.0)
         for u in range(2):
             nc.scalar.activation(out=b_pairs[u][:, 2 * SLOTS :], in_=pages[0][:, : SPARE[u]], func=ACT.Sigmoid)
 
-        def pick(table, offsets, dtype, name, tag=None):
-            picked = keep.tile([P, SLOTS], dtype, name=name, tag=tag or name, align_bytes=64)
-            nc.vector.tensor_copy(picked[:], table[:].indirect(offsets[:]))
+        def pick(table, entries, dtype, name, tag=None):
+            picked = tile([P, SLOTS], dtype, name, tag)
+            nc.vector.tensor_copy(picked[:], table[:].indirect(entries[:]))
             return picked
 
-        def look_gate(t, gate):
-            nc.scalar.activation(
-                out=gate, in_=tg_tiles[t][:].indirect(tg_list[:]), func=ACT.Sigmoid,
-                bias=offset[:, t : t + 1], scale=slope[:, t : t + 1],
+        xo_bytes = pick(xo_plane, xo_list, U8, "xo_bytes", "after_b1")
+        xo_codes = pick(xo_tab, xo_list, U32, "xo_codes", "after_b0")
+
+        w_codes = [tile([P, 2 * P], U32, "w_codes%d" % u) for u in range(2)]
+        w_bytes = [tile([P, 2 * P], U8, "w_bytes%d" % u) for u in range(2)]
+        for u in range(2):
+            pair = slice(2 * u, 2 * u + 2)
+            nc.scalar.copy(
+                w_codes[u][:].rearrange("p (t c i) -> p c t i", t=2, i=LINE // 4),
+                w_tab[:].rearrange("p (c i t) -> p c t i", t=PACK, i=LINE // 4)[:, :, pair, :],
             )
-
-        xo_codes = pick(xo_tab, xo_list, U32, "xo_codes")
-        xo_bytes = pick(xo_plane, xo_list, U8, "xo_bytes")
-
-        w_codes = keep.tile([P, HIDDEN], U32, name="w_codes", align_bytes=64)
-        w_bytes = keep.tile([P, HIDDEN], U8, name="w_bytes", align_bytes=64)
-        nc.vector.tensor_copy(
-            w_codes[:].rearrange("p (t c i) -> p c t i", t=PACK, i=4),
-            w_tab[:].rearrange("p (c i t) -> p c t i", t=PACK, i=4),
-        )
-        nc.vector.tensor_copy(
-            w_bytes[:].rearrange("p (t c i) -> p c t i", t=PACK, i=16),
-            w_plane[:].rearrange("p (c i t) -> p c t i", t=PACK, i=16),
-        )
+            nc.vector.tensor_copy(
+                w_bytes[u][:].rearrange("p (t c i) -> p c t i", t=2, i=LINE),
+                w_plane[:].rearrange("p (c i t) -> p c t i", t=PACK, i=LINE)[:, :, pair, :],
+            )
 
         def first_product(codes, scale_bytes, name):
             banks = [psum.tile([P, 2, SLOTS], F32, name="%s%d" % (name, u)) for u in range(2)]
             for t in range(PACK):
+                cols = slice(t % 2 * P, (t % 2 + 1) * P)
                 nc.tensor.matmul_mx(
                     out=banks[t // 2][:, t % 2, :],
-                    lhsT=w_codes[:, t * P : (t + 1) * P].bitcast(E4M3),
-                    lhsT_scale=w_bytes[:, t * P : (t + 1) * P],
+                    lhsT=w_codes[t // 2][:, cols].bitcast(E4M3),
+                    lhsT_scale=w_bytes[t // 2][:, cols],
                     rhs=codes, rhs_scale=scale_bytes[:], start=True, stop=True,
                 )
             return banks
@@ -144,62 +148,65 @@ def tile_list_tablepartner_oneforboth_store_scattered_kernel(
         xt_bytes = pick(xt_plane, xt_list, U8, "xt_bytes")
         a_banks = first_product(xt_codes[:].bitcast(E2M1), xt_bytes, "a_bank")
 
-        hid = keep.tile([P, SLOTS, PACK], BF16, name="hid", align_bytes=64)
-        partners, diffs, sizes, gates = [], [], [], []
+        partners = [tile([P, 2, SLOTS], F32, "partner%d" % u, ("after_sub", "after_xt")[u]) for u in range(2)]
         for u in range(2):
-            partner = keep.tile([P, 2, SLOTS], F32, name="partner%d" % u, tag="partner%d" % u, align_bytes=64)
             for e in range(2):
-                width = SLOTS + SPARE[u] if e else 2 * SLOTS
+                width = SLOTS + (SLOTS, SPARE[u])[e]
                 window = b_pairs[u][:, e * SLOTS : e * SLOTS + width].indirect(partner_list[:])
-                if u:
-                    nc.scalar.activation(out=partner[:, e, :], in_=window, func=ACT.Copy)
+                if u == 0:
+                    nc.scalar.activation(out=partners[u][:, e, :], in_=window, func=ACT.Copy)
                 else:
-                    nc.vector.tensor_copy(partner[:, e, :], window)
-            partners.append(partner)
-        for u in range(2):
-            diff = keep.tile([P, 2, SLOTS], F32, name="diff%d" % u)
-            nc.vector.tensor_tensor(diff[:], a_banks[u][:], partners[u][:], ALU.subtract)
-            diffs.append(diff)
-        for u in range(2):
-            gate = keep.tile([P, 2, SLOTS], F32, name="gate%d" % u, tag=GATE_TAG[u], align_bytes=64)
-            for e in range(2):
-                look_gate(2 * u + e, gate[:, e, :])
-            gates.append(gate)
-            size = keep.tile([P, 2, SLOTS], F32, name="size%d" % u)
-            nc.scalar.activation(out=size[:], in_=diffs[u][:], func=ACT.Abs)
-            sizes.append(size)
+                    nc.vector.tensor_copy(partners[u][:, e, :], window)
 
-        vs_codes = pick(vs_tab, vs_list, U16, "vs_codes", "partner0")
-        vs_bytes = pick(vs_plane, vs_list, U8, "vs_bytes", "xt_bytes")
-
+        diffs = [tile([P, 2, SLOTS], F32, "diff%d" % u) for u in range(2)]
         for u in range(2):
-            nc.vector.tensor_tensor(
-                hid[:, :, 2 * u : 2 * u + 2],
-                sizes[u][:].rearrange("p t j -> p j t"),
-                gates[u][:].rearrange("p t j -> p j t"),
-                ALU.mult,
+            nc.vector.tensor_tensor(diffs[u][:], a_banks[u][:], partners[u][:], ALU.subtract)
+
+        gates = [tile([P, 2, SLOTS], F32, "gate%d" % u, "after_b%d" % u) for u in range(2)]
+        for t in range(PACK):
+            nc.scalar.activation(
+                out=gates[t // 2][:, t % 2, :], in_=tg_tiles[t][:].indirect(tg_list[:]), func=ACT.Sigmoid,
+                bias=shift[:, t : t + 1], scale=slope[:, t : t + 1],
             )
 
-        hid_codes = keep.tile([P, SLOTS], U32, name="hid_codes", align_bytes=64)
-        hid_bytes = keep.tile([P, SLOTS], U8, name="hid_bytes", align_bytes=64)
-        nc.vector.quantize_mx(
-            out=hid_codes[:].bitcast(E5M2), scales=hid_bytes[:], in_=hid[:].rearrange("p j t -> p (j t)")
-        )
+        vs_codes = pick(vs_tab, vs_list, U16, "vs_codes", "after_sub")
+        vs_bytes = pick(vs_plane, vs_list, U8, "vs_bytes", "after_xt")
 
-        for h in range(2):
-            rows = slice(h * P, (h + 1) * P)
-            p_bank = psum.tile([P, SLOTS], F32, name="p_bank%d" % h)
-            nc.tensor.matmul_mx(
-                out=p_bank[:], lhsT=vs_codes[:, rows].bitcast(E2M1), lhsT_scale=vs_bytes[:, rows],
-                rhs=hid_codes[:].bitcast(E5M2), rhs_scale=hid_bytes[:], start=True, stop=True,
+        signed = tile([P, PACK, SLOTS], F32, "signed", "after_vs")
+        nc.vector.tensor_tensor(signed[:, 0:2, :], diffs[0][:], gates[0][:], ALU.mult)
+        for e in range(2):
+            nc.vector.tensor_tensor(signed[:, 2 + e, :], diffs[1][:, e, :], gates[1][:, e, :], ALU.mult)
+
+        hids = [tile([P, HALF, PACK], BF16, "hid%d" % c) for c in range(2)]
+        for c in range(2):
+            nc.scalar.activation(
+                out=hids[c][:].rearrange("p (s i) t -> p s t i", i=LINE // 4),
+                in_=signed[:, :, c * HALF : (c + 1) * HALF].rearrange("p t (s i) -> p s t i", i=LINE // 4),
+                func=ACT.Abs,
             )
-            result = keep.tile([P, SLOTS], F32, name="result%d" % h)
-            placed = pages[h][:].indirect(page_list[:])
-            if h == 0:
-                nc.vector.tensor_copy(result[:], p_bank[:])
-                nc.vector.tensor_copy(placed, result[:])
-                nc.sync.dma_start(out[rows, :], pages[h][:])
-            else:
-                nc.scalar.copy(result[:], p_bank[:])
-                nc.scalar.activation(out=placed, in_=result[:], func=ACT.Copy)
-                nc.scalar.dma_start(out[rows, :], pages[h][:])
+
+        p_banks = {}
+        for c in range(2):
+            hid_codes = tile([P, HALF], U32, "hid_codes%d" % c)
+            hid_bytes = tile([P, HALF], U8, "hid_bytes%d" % c)
+            nc.vector.quantize_mx(
+                out=hid_codes[:].bitcast(E5M2), scales=hid_bytes[:], in_=hids[c][:].rearrange("p j t -> p (j t)")
+            )
+            for h in range(2):
+                rows = slice(h * P, (h + 1) * P)
+                bank = psum.tile([P, HALF], F32, name="p_bank%d%d" % (c, h))
+                nc.tensor.matmul_mx(
+                    out=bank[:], lhsT=vs_codes[:, rows].bitcast(E2M1), lhsT_scale=vs_bytes[:, rows],
+                    rhs=hid_codes[:].bitcast(E5M2), rhs_scale=hid_bytes[:], start=True, stop=True,
+                )
+                p_banks[c, h] = bank
+
+        for c in range(2):
+            places = page_list[:, c * HALF // 16 : (c + 1) * HALF // 16]
+            results = [tile([P, HALF], F32, "result%d%d" % (c, h)) for h in range(2)]
+            nc.vector.tensor_copy(results[0][:], p_banks[c, 0][:])
+            nc.vector.tensor_copy(pages[0][:].indirect(places), results[0][:])
+            nc.scalar.copy(results[1][:], p_banks[c, 1][:])
+            nc.scalar.activation(out=pages[1][:].indirect(places), in_=results[1][:], func=ACT.Copy)
+        nc.sync.dma_start(out[:P, :], pages[0][:])
+        nc.scalar.dma_start(out[P:, :], pages[1][:])

from contextlib import ExitStack

import concourse.mybir as mybir

F32 = mybir.dt.float32
BF16 = mybir.dt.bfloat16
I32 = mybir.dt.int32
U32 = mybir.dt.uint32
U16 = mybir.dt.uint16
U8 = mybir.dt.uint8
E4M3 = mybir.dt.float8_e4m3fn_x4
E5M2 = mybir.dt.float8_e5m2_x4
E2M1 = mybir.dt.float4_e2m1fn_x4
ACT = mybir.ActivationFunctionType
ALU = mybir.AluOpType

P = 128
PACK = 4
FEATURES = 512
TABLE = 1024
SLOTS = 256
HIDDEN = 512
OUT_ROWS = 256
HALF = SLOTS // 2
LINE = 16
SPARE = (SLOTS, 96)
PAGE_CUT = TABLE // 2 - 1
FLOPS = 2 * 2 * FEATURES * HIDDEN * SLOTS + 2 * HIDDEN * OUT_ROWS * SLOTS


def tile_list_tablepartner_oneforboth_store_scattered_kernel(
    tc, xt_words, xt_scales, xo_words, xo_scales, w_words, w_scales, tg, sg, bg,
    vs_words, vs_scales, offs, offs2, offs3, offs4, offs5, offs6, out,
):
    nc = tc.nc
    with ExitStack() as ctx:
        lists = ctx.enter_context(tc.tile_pool(name="lists", bufs=1))
        keep = ctx.enter_context(tc.tile_pool(name="keep", bufs=1))
        psum = ctx.enter_context(tc.psum_pool(name="psum", bufs=1))

        def tile(shape, dtype, name, tag=None):
            return keep.tile(shape, dtype, name=name, tag=tag or name, align_bytes=64)

        def load_list(source, name):
            entries = lists.tile([P, SLOTS // 16], U16, name=name)
            nc.sync.dma_start(entries[:], source)
            return entries

        def zeroed_plane(width, name, engine, tag=None):
            plane = tile([P, width], U8, name, tag)
            engine.memset(plane[:].bitcast(I32), 0)
            return plane

        def load_scale_rows(plane, source):
            for quad in range(4):
                nc.sync.dma_start(
                    plane[32 * quad : 32 * quad + 4, :].bitcast(I32),
                    source[0, 4 * quad : 4 * quad + 4, :].bitcast(I32),
                )

        def load_words(table, source):
            nc.sync.dma_start(table[:].bitcast(I32), source.bitcast(I32))

        xo_plane = zeroed_plane(TABLE, "xo_plane", nc.gpsimd)
        w_plane = zeroed_plane(HIDDEN, "w_plane", nc.gpsimd)
        xt_plane = zeroed_plane(TABLE, "xt_plane", nc.vector, "after_xt")
        vs_plane = zeroed_plane(TABLE, "vs_plane", nc.vector)

        tg_rows = tg.rearrange("(p t) q -> t p q", t=PACK)
        tg_tiles = [tile([P, TABLE], F32, "tg%d" % t) for t in range(PACK)]
        slope = tile([P, PACK], F32, "slope")
        shift = tile([P, PACK], F32, "shift")
        nc.gpsimd.dma_start(slope[:], sg.rearrange("(p t) o -> p (t o)", t=PACK))
        nc.gpsimd.dma_start(shift[:], bg.rearrange("(p t) o -> p (t o)", t=PACK))

        xo_tab = tile([P, TABLE], U32, "xo_tab")
        w_tab = tile([P, HIDDEN], U32, "w_tab")
        xt_tab = tile([P, TABLE], U16, "xt_tab")
        vs_tab = tile([P, TABLE], U16, "vs_tab", "after_vs")

        xo_list = load_list(offs2, "xo_list")
        load_scale_rows(xo_plane, xo_scales)
        load_words(xo_tab, xo_words[0].rearrange("p n t -> p (n t)"))
        load_words(w_tab, w_words[0].rearrange("p n t -> p (n t)"))
        xt_list = load_list(offs, "xt_list")
        load_scale_rows(w_plane, w_scales)
        nc.sync.dma_start(tg_tiles[0][:], tg_rows[0])
        load_words(xt_tab, xt_words[0])
        partner_list = load_list(offs3, "partner_list")
        load_scale_rows(xt_plane, xt_scales)
        nc.sync.dma_start(tg_tiles[1][:], tg_rows[1])
        tg_list = load_list(offs4, "tg_list")
        nc.sync.dma_start(tg_tiles[2][:], tg_rows[2])
        load_words(vs_tab, vs_words[0])
        vs_list = load_list(offs5, "vs_list")
        load_scale_rows(vs_plane, vs_scales)
        nc.sync.dma_start(tg_tiles[3][:], tg_rows[3])
        page_list = load_list(offs6, "page_list")

        b_pairs = [tile([P, 2 * SLOTS + SPARE[u]], F32, "b_pair%d" % u) for u in range(2)]
        pages = [tile([P, TABLE], F32, "page%d" % h) for h in range(2)]
        for h in range(2):
            nc.vector.memset(pages[h][:, :PAGE_CUT], 0.0)
            nc.vector.memset(pages[h][:, PAGE_CUT:], 0.0)
        for u in range(2):
            nc.scalar.activation(out=b_pairs[u][:, 2 * SLOTS :], in_=pages[0][:, : SPARE[u]], func=ACT.Sigmoid)

        def pick(table, entries, dtype, name, tag=None):
            picked = tile([P, SLOTS], dtype, name, tag)
            nc.vector.tensor_copy(picked[:], table[:].indirect(entries[:]))
            return picked

        xo_bytes = pick(xo_plane, xo_list, U8, "xo_bytes", "after_b1")
        xo_codes = pick(xo_tab, xo_list, U32, "xo_codes", "after_b0")

        w_codes = [tile([P, 2 * P], U32, "w_codes%d" % u) for u in range(2)]
        w_bytes = [tile([P, 2 * P], U8, "w_bytes%d" % u) for u in range(2)]
        for u in range(2):
            pair = slice(2 * u, 2 * u + 2)
            nc.scalar.copy(
                w_codes[u][:].rearrange("p (t c i) -> p c t i", t=2, i=LINE // 4),
                w_tab[:].rearrange("p (c i t) -> p c t i", t=PACK, i=LINE // 4)[:, :, pair, :],
            )
            nc.vector.tensor_copy(
                w_bytes[u][:].rearrange("p (t c i) -> p c t i", t=2, i=LINE),
                w_plane[:].rearrange("p (c i t) -> p c t i", t=PACK, i=LINE)[:, :, pair, :],
            )

        def first_product(codes, scale_bytes, name):
            banks = [psum.tile([P, 2, SLOTS], F32, name="%s%d" % (name, u)) for u in range(2)]
            for t in range(PACK):
                cols = slice(t % 2 * P, (t % 2 + 1) * P)
                nc.tensor.matmul_mx(
                    out=banks[t // 2][:, t % 2, :],
                    lhsT=w_codes[t // 2][:, cols].bitcast(E4M3),
                    lhsT_scale=w_bytes[t // 2][:, cols],
                    rhs=codes, rhs_scale=scale_bytes[:], start=True, stop=True,
                )
            return banks

        b_banks = first_product(xo_codes[:].bitcast(E4M3), xo_bytes, "b_bank")
        for u in range(2):
            nc.scalar.activation(
                out=b_pairs[u][:, : 2 * SLOTS], in_=b_banks[u][:].rearrange("p t j -> p (t j)"), func=ACT.Copy
            )

        xt_codes = pick(xt_tab, xt_list, U16, "xt_codes")
        xt_bytes = pick(xt_plane, xt_list, U8, "xt_bytes")
        a_banks = first_product(xt_codes[:].bitcast(E2M1), xt_bytes, "a_bank")

        partners = [tile([P, 2, SLOTS], F32, "partner%d" % u, ("after_sub", "after_xt")[u]) for u in range(2)]
        for u in range(2):
            for e in range(2):
                width = SLOTS + (SLOTS, SPARE[u])[e]
                window = b_pairs[u][:, e * SLOTS : e * SLOTS + width].indirect(partner_list[:])
                if u == 0:
                    nc.scalar.activation(out=partners[u][:, e, :], in_=window, func=ACT.Copy)
                else:
                    nc.vector.tensor_copy(partners[u][:, e, :], window)

        diffs = [tile([P, 2, SLOTS], F32, "diff%d" % u) for u in range(2)]
        for u in range(2):
            nc.vector.tensor_tensor(diffs[u][:], a_banks[u][:], partners[u][:], ALU.subtract)

        gates = [tile([P, 2, SLOTS], F32, "gate%d" % u, "after_b%d" % u) for u in range(2)]
        for t in range(PACK):
            nc.scalar.activation(
                out=gates[t // 2][:, t % 2, :], in_=tg_tiles[t][:].indirect(tg_list[:]), func=ACT.Sigmoid,
                bias=shift[:, t : t + 1], scale=slope[:, t : t + 1],
            )

        vs_codes = pick(vs_tab, vs_list, U16, "vs_codes", "after_sub")
        vs_bytes = pick(vs_plane, vs_list, U8, "vs_bytes", "after_xt")

        signed = tile([P, PACK, SLOTS], F32, "signed", "after_vs")
        nc.vector.tensor_tensor(signed[:, 0:2, :], diffs[0][:], gates[0][:], ALU.mult)
        for e in range(2):
            nc.vector.tensor_tensor(signed[:, 2 + e, :], diffs[1][:, e, :], gates[1][:, e, :], ALU.mult)

        hids = [tile([P, HALF, PACK], BF16, "hid%d" % c) for c in range(2)]
        for c in range(2):
            nc.scalar.activation(
                out=hids[c][:].rearrange("p (s i) t -> p s t i", i=LINE // 4),
                in_=signed[:, :, c * HALF : (c + 1) * HALF].rearrange("p t (s i) -> p s t i", i=LINE // 4),
                func=ACT.Abs,
            )

        p_banks = {}
        for c in range(2):
            hid_codes = tile([P, HALF], U32, "hid_codes%d" % c)
            hid_bytes = tile([P, HALF], U8, "hid_bytes%d" % c)
            nc.vector.quantize_mx(
                out=hid_codes[:].bitcast(E5M2), scales=hid_bytes[:], in_=hids[c][:].rearrange("p j t -> p (j t)")
            )
            for h in range(2):
                rows = slice(h * P, (h + 1) * P)
                bank = psum.tile([P, HALF], F32, name="p_bank%d%d" % (c, h))
                nc.tensor.matmul_mx(
                    out=bank[:], lhsT=vs_codes[:, rows].bitcast(E2M1), lhsT_scale=vs_bytes[:, rows],
                    rhs=hid_codes[:].bitcast(E5M2), rhs_scale=hid_bytes[:], start=True, stop=True,
                )
                p_banks[c, h] = bank

        for c in range(2):
            places = page_list[:, c * HALF // 16 : (c + 1) * HALF // 16]
            results = [tile([P, HALF], F32, "result%d%d" % (c, h)) for h in range(2)]
            nc.vector.tensor_copy(results[0][:], p_banks[c, 0][:])
            nc.vector.tensor_copy(pages[0][:].indirect(places), results[0][:])
            nc.scalar.copy(results[1][:], p_banks[c, 1][:])
            nc.scalar.activation(out=pages[1][:].indirect(places), in_=results[1][:], func=ACT.Copy)
        nc.sync.dma_start(out[:P, :], pages[0][:])
        nc.scalar.dma_start(out[P:, :], pages[1][:])
